import numpy as np
import ml_dtypes


def mxq(x, axis, fmt="e4m3"):
    dtype, down = {"e4m3": (ml_dtypes.float8_e4m3fn, 7), "e5m2": (ml_dtypes.float8_e5m2, 14)}[fmt]
    v = np.moveaxis(np.asarray(x, np.float32).astype(ml_dtypes.bfloat16).astype(np.float64), axis, -1)
    blocks = v.reshape(v.shape[:-1] + (-1, 32))
    amax = np.abs(blocks).max(-1, keepdims=True)
    byte = np.maximum(np.where(amax > 0, np.frexp(amax)[1] - 1 + 127, 0) - down, 1)
    scale = np.exp2(byte - 127.0)
    codes = (blocks / scale).astype(np.float32).astype(dtype).astype(np.float64)
    return np.moveaxis((codes * scale).reshape(v.shape), -1, axis)


WIDE = False


def mx_kscale(k):
    if not WIDE:
        return np.ones(k)
    levels = np.array([30, -30])
    if k % 512:
        return np.exp2(np.random.permutation(np.resize(levels, k // 32))).repeat(32)
    a = np.empty((k // 512, 16))
    for p in range(k // 512):
        a[p, :8] = np.random.permutation(np.resize(levels, 8))
        for g in range(8):
            far = levels[np.abs(levels - a[p, g]) >= 10]
            a[p, g + 8] = far[np.random.randint(len(far))]
    return np.exp2(a.ravel()).repeat(32)


def f64(x):
    return np.asarray(x).astype(np.float64)


def striped(idx):
    return np.tile(np.asarray(idx).reshape(-1, 16).T, (8, 1)).astype(np.uint16)


def unstriped(offs):
    return offs[:16].T.reshape(-1).astype(np.int64)


E2M1 = np.array([0.0, 0.5, 1.0, 1.5, 2.0, 3.0, 4.0, 6.0, -0.0, -0.5, -1.0, -1.5, -2.0, -3.0, -4.0, -6.0])


def pack_weight(w, fmt):
    k, n = w.shape
    w = f64(np.asarray(w, np.float32).astype(ml_dtypes.bfloat16)).reshape(k // 32, 32, n)
    amax = np.abs(w).max(1)
    if fmt == "e4m3":
        byte = np.frexp(amax)[1] - 1 + 127 - 7
    else:
        mant, ex = np.frexp(amax / 6.0)
        byte = np.where(mant > 0.5, ex, ex - 1) + 127
    byte = np.clip(np.where(amax > 0, byte, 1), 1, 254)
    scaled = (w * np.exp2(127.0 - byte)[:, None, :]).reshape(k, n).astype(np.float32)
    by_word = np.ascontiguousarray(scaled.reshape(k // 512, 128, 4, n).transpose(0, 1, 3, 2))
    if fmt == "e4m3":
        words = by_word.astype(ml_dtypes.float8_e4m3fn).view(np.uint8)
    else:
        c = by_word.astype(ml_dtypes.float4_e2m1fn).view(np.uint8) & 0xF
        words = (c[..., 0::2] | (c[..., 1::2] << 4)).reshape(k // 512, 128, 2 * n)
    return np.ascontiguousarray(words), np.ascontiguousarray(byte.astype(np.uint8).reshape(k // 512, 16, n))


def unpack_weight(words, scales, fmt):
    g, _, n = scales.shape
    words = np.ascontiguousarray(words).reshape(g, 128, n, -1)
    if fmt == "e4m3":
        vals = words.view(ml_dtypes.float8_e4m3fn).astype(np.float64)
    else:
        nib = np.empty((g, 128, n, 4), np.uint8)
        nib[..., 0::2] = words & 0xF
        nib[..., 1::2] = words >> 4
        vals = E2M1[nib]
    vals = vals * np.repeat(np.exp2(scales.astype(np.float64) - 127.0), 8, axis=1)[..., None]
    return vals.transpose(0, 1, 3, 2).reshape(g * 512, n)


K, T, J, R, O, N = 1024, 1024, 256, 512, 128, 256


def setup_inputs():
    n = np.random.standard_normal
    idx = np.random.permutation(T)[:J]
    idx2 = np.random.permutation(T)[:J]
    idx3 = np.random.permutation(J)[:O]
    fk = mx_kscale(K)
    fr = mx_kscale(R)
    wp = pack_weight(n((K, R)) * 1 / np.sqrt(K) * fk[:, None] * fr, "e2m1")
    wbp = pack_weight(n((R, N)) * 1 / np.sqrt(R) / fr[:, None], "e4m3")
    return {
        "xf": (n((K, T))).astype(np.float32),
        "fk": (np.random.uniform(0.5, 2.0, (K, 1)) / fk[:, None]).astype(np.float32),
        "w_words": wp[0],
        "w_scales": wp[1],
        "wb_words": wbp[0],
        "wb_scales": wbp[1],
        "rs": (1.0 * n((O, N))).astype(np.float32),
        "offs": striped(idx),
        "offs2": striped(idx2),
        "offs3": striped(idx3),
    }


def reference(xf, fk, w_words, w_scales, wb_words, wb_scales, rs, offs, offs2, offs3):
    idx = unstriped(offs)
    idx2 = unstriped(offs2)
    idx3 = unstriped(offs3)
    wu = unpack_weight(w_words, w_scales, "e2m1")
    wbu = unpack_weight(wb_words, wb_scales, "e4m3")
    u = np.maximum(f64(xf)[:, idx], f64(xf)[:, idx2]) * f64(fk)
    uq = mxq(u, 0, "e4m3")
    a = wu.T @ uq
    ha = np.maximum(a, 0.0)
    hid = ha[:, idx3]
    hidq = mxq(hid, 0, "e5m2")
    p = hidq.T @ wbu
    pk2 = np.max(np.abs(p), axis=1, keepdims=True)
    y = p / (pk2 + 0.2) + 0.3 * f64(rs)
    return y

@@ -1,0 +1,175 @@
+from contextlib import ExitStack
+
+import concourse.mybir as mybir
+
+K, T, J, R, O, N = 1024, 1024, 256, 512, 128, 256
+FLOPS = 2 * K * R * J + 2 * R * O * N
+
+F32 = mybir.dt.float32
+BF16 = mybir.dt.bfloat16
+I32 = mybir.dt.int32
+U32 = mybir.dt.uint32
+U16 = mybir.dt.uint16
+U8 = mybir.dt.uint8
+E4M3 = mybir.dt.float8_e4m3fn_x4
+E5M2 = mybir.dt.float8_e5m2_x4
+E2M1 = mybir.dt.float4_e2m1fn_x4
+ALU = mybir.AluOpType
+ACT = mybir.ActivationFunctionType
+
+P = 128
+PACK = 4
+PASSES = K // (P * PACK)
+HALVES = 2
+JH = J // HALVES
+STRIPE = 16
+
+
+def tile_list_largerpicks_relooked_rowpeaks_kernel(
+    tc, xf, fk, w_words, w_scales, wb_words, wb_scales, rs, offs, offs2, offs3, out
+):
+    nc = tc.nc
+    with ExitStack() as ctx:
+        sb = ctx.enter_context(tc.tile_pool(name="sb", bufs=1))
+        psum = ctx.enter_context(tc.psum_pool(name="psum", bufs=1))
+
+        list1 = sb.tile([P, J // STRIPE], U16, name="list1")
+        list2 = sb.tile([P, J // STRIPE], U16, name="list2")
+        list3 = sb.tile([P, O // STRIPE], U16, name="list3")
+        planes = [(a, t) for a in range(PASSES) for t in range(PACK)]
+        x_rows = xf.rearrange("(a p t) c -> a t p c", a=PASSES, t=PACK)
+        x = {at: sb.tile([P, T], F32, name="x%d%d" % at) for at in planes}
+        w_raw = sb.tile([P, PASSES, 2 * R], U8, name="w_raw", align_bytes=64)
+        wb_codes = sb.tile([P, PACK * N], U8, name="wb_codes", align_bytes=64)
+        rs_raw = sb.tile([P, N], F32, name="rs_raw")
+
+        def load_plane(at):
+            nc.sync.dma_start(x[at][:], x_rows[at[0], at[1]])
+
+        factor = sb.tile([P, PASSES, PACK], F32, name="factor")
+        nc.scalar.dma_start(factor[:], fk.rearrange("(a p t) o -> p a (t o)", a=PASSES, t=PACK))
+        ws_raw = sb.tile([P, PASSES, R], U8, name="ws_raw", align_bytes=64)
+        wb_plane = sb.tile([P, N], U8, name="wb_plane", align_bytes=64)
+        nc.vector.memset(ws_raw[:].bitcast(I32), 0)
+        nc.vector.memset(wb_plane[:].bitcast(I32), 0)
+
+        nc.sync.dma_start(list1[:], offs)
+        nc.sync.dma_start(list2[:], offs2)
+        nc.sync.dma_start(w_raw[:].bitcast(I32), w_words.rearrange("a p b -> p a b").bitcast(I32))
+        for at in planes[:2]:
+            load_plane(at)
+        for q in range(4):
+            nc.sync.dma_start(
+                ws_raw[32 * q : 32 * q + 4].bitcast(I32),
+                w_scales[:, 4 * q : 4 * q + 4, :].rearrange("a r c -> r a c").bitcast(I32),
+            )
+        for at in planes[2:]:
+            load_plane(at)
+        nc.sync.dma_start(list3[:], offs3)
+        nc.sync.dma_start(rs_raw[:], rs)
+        nc.sync.dma_start(wb_codes[:].bitcast(I32), wb_words[0].rearrange("p n t -> p (n t)").bitcast(I32))
+
+        for q in range(4):
+            nc.gpsimd.dma_start(
+                wb_plane[32 * q : 32 * q + 4].bitcast(I32), wb_scales[0, 4 * q : 4 * q + 4, :].bitcast(I32)
+            )
+
+        w_codes = sb.tile([P, PASSES, 2 * R], U8, name="w_codes", align_bytes=64)
+        w_plane = sb.tile([P, PASSES, R], U8, name="w_plane", align_bytes=64)
+        nc.vector.tensor_copy(
+            w_codes[:].bitcast(U16).rearrange("p a (t m) -> p a t m", t=PACK),
+            w_raw[:].bitcast(U16).rearrange("p a (m t) -> p a t m", t=PACK),
+        )
+        nc.vector.tensor_copy(
+            w_plane[:].rearrange("p a (t m) -> p a t m", t=PACK),
+            ws_raw[:].rearrange("p a (m t) -> p a t m", t=PACK),
+        )
+
+        def larger_picks(at, parts, outs):
+            width = J // parts
+            picks = []
+            for h in range(parts):
+                cols = slice(h * width // STRIPE, (h + 1) * width // STRIPE)
+                pick1 = sb.tile([P, width], F32, name="pick1_%d%d%d" % (at + (h,)))
+                pick2 = sb.tile([P, width], F32, name="pick2_%d%d%d" % (at + (h,)))
+                nc.scalar.activation(pick2[:], x[at][:].indirect(list2[:, cols]), ACT.Copy)
+                if h == 0 and at in on_vector:
+                    nc.vector.tensor_copy(pick1[:], x[at][:].indirect(list1[:, cols]))
+                else:
+                    nc.scalar.activation(pick1[:], x[at][:].indirect(list1[:, cols]), ACT.Copy)
+                picks.append((pick1, pick2))
+            for h in range(parts):
+                nc.vector.tensor_tensor(outs[h], picks[h][0][:], picks[h][1][:], ALU.max)
+
+        on_vector = [at for at in planes if at != (0, 2)]
+        acc = [psum.tile([P, J], F32, name="acc%d" % t) for t in range(PACK)]
+        for a in range(PASSES):
+            u = [sb.tile([P, JH, PACK], BF16, name="u%d%d" % (a, h), align_bytes=64) for h in range(HALVES)]
+            u_codes = sb.tile([P, J], U32, name="u_codes%d" % a, align_bytes=64)
+            u_plane = sb.tile([P, J], U8, name="u_plane%d" % a, align_bytes=64)
+            if a < PASSES - 1:
+                larger = sb.tile([P, PACK, J], F32, name="larger")
+                for t in range(PACK):
+                    larger_picks((a, t), 1, [larger[:, t, :]])
+                for h in range(HALVES):
+                    nc.vector.tensor_tensor(
+                        u[h][:].rearrange("p (c i) t -> p c t i", i=4),
+                        larger[:, :, h * JH : (h + 1) * JH].rearrange("p t (c i) -> p c t i", i=4),
+                        factor[:, a, :].unsqueeze(1).unsqueeze(3).broadcast_to([P, JH // 4, PACK, 4]),
+                        ALU.mult,
+                    )
+            else:
+                for t in range(PACK):
+                    halves = [sb.tile([P, JH], F32, name="larger%d%d" % (t, h))[:] for h in range(HALVES)]
+                    larger_picks((a, t), HALVES, halves)
+                    for h in range(HALVES):
+                        nc.vector.tensor_scalar(u[h][:, :, t], halves[h], factor[:, a, t : t + 1], None, ALU.mult)
+            for h in range(HALVES):
+                cols = slice(h * JH, (h + 1) * JH)
+                nc.vector.quantize_mx(
+                    u_codes[:, cols].bitcast(E4M3), u_plane[:, cols], u[h][:].rearrange("p j t -> p (j t)")
+                )
+            for t in range(PACK):
+                nc.tensor.matmul_mx(
+                    acc[t][:],
+                    lhsT=w_codes[:, a, 2 * P * t : 2 * P * (t + 1)].bitcast(E2M1),
+                    lhsT_scale=w_plane[:, a, P * t : P * (t + 1)],
+                    rhs=u_codes[:].bitcast(E4M3),
+                    rhs_scale=u_plane[:],
+                    start=(a == 0),
+                    stop=(a == PASSES - 1),
+                )
+
+        residual = sb.tile([P, N], F32, name="residual")
+        nc.scalar.activation(residual[:], rs_raw[:], ACT.Copy, scale=0.3)
+
+        hid = sb.tile([P, O, PACK], BF16, name="hid", align_bytes=64)
+        for t in range(PACK):
+            ha = sb.tile([P, J], F32, name="ha%d" % t)
+            nc.scalar.activation(ha[:], acc[t][:], ACT.Relu)
+            nc.vector.tensor_copy(hid[:, :, t], ha[:].indirect(list3[:]))
+        hid_codes = sb.tile([P, O], U32, name="hid_codes", align_bytes=64)
+        hid_plane = sb.tile([P, O], U8, name="hid_plane", align_bytes=64)
+        nc.vector.quantize_mx(hid_codes[:].bitcast(E5M2), hid_plane[:], hid[:].rearrange("p o t -> p (o t)"))
+
+        prod = psum.tile([P, N], F32, name="prod")
+        nc.tensor.matmul_mx(
+            prod[:],
+            lhsT=hid_codes[:].bitcast(E5M2),
+            lhsT_scale=hid_plane[:],
+            rhs=wb_codes[:].bitcast(U32).bitcast(E4M3),
+            rhs_scale=wb_plane[:],
+            start=True,
+            stop=True,
+        )
+        top = sb.tile([P, 1], F32, name="top")
+        bottom = sb.tile([P, 1], F32, name="bottom")
+        nc.vector.tensor_reduce(top[:], prod[:], mybir.AxisListType.X, ALU.max)
+        nc.vector.tensor_reduce(bottom[:], prod[:], mybir.AxisListType.X, ALU.min, negate=True)
+        denom = sb.tile([P, 1], F32, name="denom")
+        nc.vector.tensor_scalar(denom[:], bottom[:], top[:], 0.2, ALU.max, ALU.add)
+        inv = sb.tile([P, 1], F32, name="inv")
+        nc.vector.reciprocal(inv[:], denom[:])
+        result = sb.tile([P, N], F32, name="result")
+        nc.vector.scalar_tensor_tensor(result[:], prod[:], inv[:], residual[:], ALU.mult, ALU.add)
+        nc.sync.dma_start(out, result[:])

@@ -16,13 +16,18 @@ E5M2 = mybir.dt.float8_e5m2_x4
 E2M1 = mybir.dt.float4_e2m1fn_x4
 ALU = mybir.AluOpType
 ACT = mybir.ActivationFunctionType
+X = mybir.AxisListType.X
 
 P = 128
 PACK = 4
 PASSES = K // (P * PACK)
 HALVES = 2
 JH = J // HALVES
+NH = N // HALVES
 STRIPE = 16
+JOINT = [3,3]
+REUSE = {"pick1_01":"pick2_00","pick1_02":"pick1_00","late03":"pick2_02","early1":"pick2_02","pick1_11":"u0","late13":"pick2_12"}
+SHARE = [256,256,128,0,0,256,0,0]
 
 
 def tile_list_largerpicks_relooked_rowpeaks_kernel(
@@ -42,103 +47,115 @@ def tile_list_largerpicks_relooked_rowpeaks_kernel(
         w_raw = sb.tile([P, PASSES, 2 * R], U8, name="w_raw", align_bytes=64)
         wb_codes = sb.tile([P, PACK * N], U8, name="wb_codes", align_bytes=64)
         rs_raw = sb.tile([P, N], F32, name="rs_raw")
+        factor = sb.tile([P, PASSES, PACK], F32, name="factor")
+        ws_raw = sb.tile([P, PASSES, R], U8, name="ws_raw", align_bytes=64)
+        wb_plane = sb.tile([P, N], U8, name="wb_plane", align_bytes=64)
+
+        def tile(shape, dtype, name):
+            return sb.tile(shape, dtype, name=name, tag=REUSE.get(name, name), align_bytes=64)
 
         def load_plane(at):
             nc.sync.dma_start(x[at][:], x_rows[at[0], at[1]])
 
-        factor = sb.tile([P, PASSES, PACK], F32, name="factor")
-        nc.scalar.dma_start(factor[:], fk.rearrange("(a p t) o -> p a (t o)", a=PASSES, t=PACK))
-        ws_raw = sb.tile([P, PASSES, R], U8, name="ws_raw", align_bytes=64)
-        wb_plane = sb.tile([P, N], U8, name="wb_plane", align_bytes=64)
+        warm_in = sb.tile([P, 1], F32, name="warm_in")
+        warm_out = sb.tile([P, 1], F32, name="warm_out")
+        nc.vector.memset(warm_in[:], 0.0)
+        nc.scalar.activation(warm_out[:], warm_in[:], ACT.Copy)
         nc.vector.memset(ws_raw[:].bitcast(I32), 0)
         nc.vector.memset(wb_plane[:].bitcast(I32), 0)
 
         nc.sync.dma_start(list1[:], offs)
         nc.sync.dma_start(list2[:], offs2)
+        load_plane(planes[0])
         nc.sync.dma_start(w_raw[:].bitcast(I32), w_words.rearrange("a p b -> p a b").bitcast(I32))
-        for at in planes[:2]:
-            load_plane(at)
         for q in range(4):
             nc.sync.dma_start(
                 ws_raw[32 * q : 32 * q + 4].bitcast(I32),
                 w_scales[:, 4 * q : 4 * q + 4, :].rearrange("a r c -> r a c").bitcast(I32),
             )
-        for at in planes[2:]:
+        nc.sync.dma_start(factor[:], fk.rearrange("(a p t) o -> p a (t o)", a=PASSES, t=PACK))
+        for at in planes[1:]:
             load_plane(at)
         nc.sync.dma_start(list3[:], offs3)
         nc.sync.dma_start(rs_raw[:], rs)
         nc.sync.dma_start(wb_codes[:].bitcast(I32), wb_words[0].rearrange("p n t -> p (n t)").bitcast(I32))
 
         for q in range(4):
-            nc.gpsimd.dma_start(
+            nc.sync.dma_start(
                 wb_plane[32 * q : 32 * q + 4].bitcast(I32), wb_scales[0, 4 * q : 4 * q + 4, :].bitcast(I32)
             )
 
         w_codes = sb.tile([P, PASSES, 2 * R], U8, name="w_codes", align_bytes=64)
         w_plane = sb.tile([P, PASSES, R], U8, name="w_plane", align_bytes=64)
-        nc.vector.tensor_copy(
-            w_codes[:].bitcast(U16).rearrange("p a (t m) -> p a t m", t=PACK),
-            w_raw[:].bitcast(U16).rearrange("p a (m t) -> p a t m", t=PACK),
-        )
-        nc.vector.tensor_copy(
-            w_plane[:].rearrange("p a (t m) -> p a t m", t=PACK),
-            ws_raw[:].rearrange("p a (m t) -> p a t m", t=PACK),
-        )
 
-        def larger_picks(at, parts, outs):
-            width = J // parts
-            picks = []
-            for h in range(parts):
-                cols = slice(h * width // STRIPE, (h + 1) * width // STRIPE)
-                pick1 = sb.tile([P, width], F32, name="pick1_%d%d%d" % (at + (h,)))
-                pick2 = sb.tile([P, width], F32, name="pick2_%d%d%d" % (at + (h,)))
-                nc.scalar.activation(pick2[:], x[at][:].indirect(list2[:, cols]), ACT.Copy)
-                if h == 0 and at in on_vector:
-                    nc.vector.tensor_copy(pick1[:], x[at][:].indirect(list1[:, cols]))
-                else:
-                    nc.scalar.activation(pick1[:], x[at][:].indirect(list1[:, cols]), ACT.Copy)
-                picks.append((pick1, pick2))
-            for h in range(parts):
-                nc.vector.tensor_tensor(outs[h], picks[h][0][:], picks[h][1][:], ALU.max)
+        def deal_weights():
+            nc.vector.tensor_copy(
+                w_codes[:].bitcast(U16).rearrange("p a (t m) -> p a t m", t=PACK),
+                w_raw[:].bitcast(U16).rearrange("p a (m t) -> p a t m", t=PACK),
+            )
+            nc.vector.tensor_copy(
+                w_plane[:].rearrange("p a (t m) -> p a t m", t=PACK),
+                ws_raw[:].rearrange("p a (m t) -> p a t m", t=PACK),
+            )
 
-        on_vector = [at for at in planes if at != (0, 2)]
+        def gather(engine_is_vector, picked, window, offsets, lo, hi):
+            source = window[:].indirect(offsets[:, lo // STRIPE : hi // STRIPE])
+            if engine_is_vector:
+                nc.vector.tensor_copy(picked[:, lo:hi], source)
+            else:
+                nc.scalar.activation(picked[:, lo:hi], source, ACT.Copy)
+
         acc = [psum.tile([P, J], F32, name="acc%d" % t) for t in range(PACK)]
         for a in range(PASSES):
-            u = [sb.tile([P, JH, PACK], BF16, name="u%d%d" % (a, h), align_bytes=64) for h in range(HALVES)]
+            u = tile([P, J, PACK], BF16, "u%d" % a)
             u_codes = sb.tile([P, J], U32, name="u_codes%d" % a, align_bytes=64)
             u_plane = sb.tile([P, J], U8, name="u_plane%d" % a, align_bytes=64)
-            if a < PASSES - 1:
-                larger = sb.tile([P, PACK, J], F32, name="larger")
-                for t in range(PACK):
-                    larger_picks((a, t), 1, [larger[:, t, :]])
-                for h in range(HALVES):
+            last_pass = a == PASSES - 1
+            joint = JOINT[a]
+            early = tile([P, joint, J], F32, "early%d" % a)
+            for t in range(PACK):
+                window = x[(a, t)]
+                pick1 = tile([P, J], F32, "pick1_%d%d" % (a, t))
+                pick2 = tile([P, J], F32, "pick2_%d%d" % (a, t))
+                larger = early[:, t, :] if t < joint else tile([P, J], F32, "late%d%d" % (a, t))[:]
+                share = SHARE[PACK * a + t]
+                parts = [(0, JH), (JH, J)] if last_pass and t == PACK - 1 else [(0, J)]
+                if share:
+                    gather(True, pick1, window, list1, 0, share)
+                for lo, hi in parts:
+                    gather(False, pick2, window, list2, lo, hi)
+                    if max(lo, share) < hi:
+                        gather(False, pick1, window, list1, max(lo, share), hi)
+                for lo, hi in parts:
+                    nc.vector.tensor_tensor(larger[:, lo:hi], pick1[:, lo:hi], pick2[:, lo:hi], ALU.max)
+                if t == joint - 1:
                     nc.vector.tensor_tensor(
-                        u[h][:].rearrange("p (c i) t -> p c t i", i=4),
-                        larger[:, :, h * JH : (h + 1) * JH].rearrange("p t (c i) -> p c t i", i=4),
-                        factor[:, a, :].unsqueeze(1).unsqueeze(3).broadcast_to([P, JH // 4, PACK, 4]),
+                        u[:, :, :joint].rearrange("p (c i) t -> p c t i", i=4),
+                        early[:].rearrange("p t (c i) -> p c t i", i=4),
+                        factor[:, a, :joint].unsqueeze(1).unsqueeze(3).broadcast_to([P, J // 4, joint, 4]),
                         ALU.mult,
                     )
-            else:
-                for t in range(PACK):
-                    halves = [sb.tile([P, JH], F32, name="larger%d%d" % (t, h))[:] for h in range(HALVES)]
-                    larger_picks((a, t), HALVES, halves)
-                    for h in range(HALVES):
-                        nc.vector.tensor_scalar(u[h][:, :, t], halves[h], factor[:, a, t : t + 1], None, ALU.mult)
-            for h in range(HALVES):
-                cols = slice(h * JH, (h + 1) * JH)
+                if t >= joint:
+                    for lo, hi in parts:
+                        nc.vector.tensor_scalar(u[:, lo:hi, t], larger[:, lo:hi], factor[:, a, t : t + 1], None, ALU.mult)
+                if (a, t) == planes[0]:
+                    deal_weights()
+            parts = [(0, JH), (JH, J)] if last_pass else [(0, J)]
+            for lo, hi in parts:
                 nc.vector.quantize_mx(
-                    u_codes[:, cols].bitcast(E4M3), u_plane[:, cols], u[h][:].rearrange("p j t -> p (j t)")
+                    u_codes[:, lo:hi].bitcast(E4M3), u_plane[:, lo:hi], u[:, lo:hi, :].rearrange("p j t -> p (j t)")
                 )
             for t in range(PACK):
-                nc.tensor.matmul_mx(
-                    acc[t][:],
-                    lhsT=w_codes[:, a, 2 * P * t : 2 * P * (t + 1)].bitcast(E2M1),
-                    lhsT_scale=w_plane[:, a, P * t : P * (t + 1)],
-                    rhs=u_codes[:].bitcast(E4M3),
-                    rhs_scale=u_plane[:],
-                    start=(a == 0),
-                    stop=(a == PASSES - 1),
-                )
+                for lo, hi in parts:
+                    nc.tensor.matmul_mx(
+                        acc[t][:, lo:hi],
+                        lhsT=w_codes[:, a, 2 * P * t : 2 * P * (t + 1)].bitcast(E2M1),
+                        lhsT_scale=w_plane[:, a, P * t : P * (t + 1)],
+                        rhs=u_codes[:, lo:hi].bitcast(E4M3),
+                        rhs_scale=u_plane[:, lo:hi],
+                        start=(a == 0),
+                        stop=(last_pass and hi == J),
+                    )
 
         residual = sb.tile([P, N], F32, name="residual")
         nc.scalar.activation(residual[:], rs_raw[:], ACT.Copy, scale=0.3)
@@ -152,24 +169,28 @@ def tile_list_largerpicks_relooked_rowpeaks_kernel(
         hid_plane = sb.tile([P, O], U8, name="hid_plane", align_bytes=64)
         nc.vector.quantize_mx(hid_codes[:].bitcast(E5M2), hid_plane[:], hid[:].rearrange("p o t -> p (o t)"))
 
-        prod = psum.tile([P, N], F32, name="prod")
-        nc.tensor.matmul_mx(
-            prod[:],
-            lhsT=hid_codes[:].bitcast(E5M2),
-            lhsT_scale=hid_plane[:],
-            rhs=wb_codes[:].bitcast(U32).bitcast(E4M3),
-            rhs_scale=wb_plane[:],
-            start=True,
-            stop=True,
-        )
-        top = sb.tile([P, 1], F32, name="top")
-        bottom = sb.tile([P, 1], F32, name="bottom")
-        nc.vector.tensor_reduce(top[:], prod[:], mybir.AxisListType.X, ALU.max)
-        nc.vector.tensor_reduce(bottom[:], prod[:], mybir.AxisListType.X, ALU.min, negate=True)
+        prod = [psum.tile([P, NH], F32, name="prod%d" % h) for h in range(HALVES)]
+        for h in range(HALVES):
+            nc.tensor.matmul_mx(
+                prod[h][:],
+                lhsT=hid_codes[:].bitcast(E5M2),
+                lhsT_scale=hid_plane[:],
+                rhs=wb_codes[:].bitcast(U32)[:, h * NH : (h + 1) * NH].bitcast(E4M3),
+                rhs_scale=wb_plane[:, h * NH : (h + 1) * NH],
+                start=True,
+                stop=True,
+            )
+        sizes = sb.tile([P, NH + 2], F32, name="sizes")
+        nc.vector.tensor_reduce(sizes[:, NH : NH + 1], prod[0][:], X, ALU.max)
+        nc.vector.tensor_reduce(sizes[:, NH + 1 : NH + 2], prod[0][:], X, ALU.min, negate=True)
+        nc.scalar.activation(sizes[:, :NH], prod[1][:], ACT.Abs)
+        shifted = sb.tile([P, NH + 2], F32, name="shifted")
         denom = sb.tile([P, 1], F32, name="denom")
-        nc.vector.tensor_scalar(denom[:], bottom[:], top[:], 0.2, ALU.max, ALU.add)
+        nc.vector.tensor_scalar(shifted[:], sizes[:], 0.2, None, ALU.add, ALU.max, accum_out=denom[:])
         inv = sb.tile([P, 1], F32, name="inv")
         nc.vector.reciprocal(inv[:], denom[:])
         result = sb.tile([P, N], F32, name="result")
-        nc.vector.scalar_tensor_tensor(result[:], prod[:], inv[:], residual[:], ALU.mult, ALU.add)
+        for h in range(HALVES):
+            cols = slice(h * NH, (h + 1) * NH)
+            nc.vector.scalar_tensor_tensor(result[:, cols], prod[h][:], inv[:], residual[:, cols], ALU.mult, ALU.add)
         nc.sync.dma_start(out, result[:])

@@ -68,10 +68,10 @@ def tile_list_largerpicks_relooked_rowpeaks_kernel(
         nc.sync.dma_start(list2[:], offs2)
         load_plane(planes[0])
         nc.sync.dma_start(w_raw[:].bitcast(I32), w_words.rearrange("a p b -> p a b").bitcast(I32))
-        for q in range(4):
+        for r in range(4):
             nc.sync.dma_start(
-                ws_raw[32 * q : 32 * q + 4].bitcast(I32),
-                w_scales[:, 4 * q : 4 * q + 4, :].rearrange("a r c -> r a c").bitcast(I32),
+                ws_raw[r:P:32].bitcast(I32),
+                w_scales[:, r:16:4, :].rearrange("a q c -> q a c").bitcast(I32),
             )
         nc.sync.dma_start(factor[:], fk.rearrange("(a p t) o -> p a (t o)", a=PASSES, t=PACK))
         for at in planes[1:]:
@@ -80,10 +80,8 @@ def tile_list_largerpicks_relooked_rowpeaks_kernel(
         nc.sync.dma_start(rs_raw[:], rs)
         nc.sync.dma_start(wb_codes[:].bitcast(I32), wb_words[0].rearrange("p n t -> p (n t)").bitcast(I32))
 
-        for q in range(4):
-            nc.sync.dma_start(
-                wb_plane[32 * q : 32 * q + 4].bitcast(I32), wb_scales[0, 4 * q : 4 * q + 4, :].bitcast(I32)
-            )
+        for r in range(4):
+            nc.sync.dma_start(wb_plane[r:P:32].bitcast(I32), wb_scales[0, r:16:4, :].bitcast(I32))
 
         w_codes = sb.tile([P, PASSES, 2 * R], U8, name="w_codes", align_bytes=64)
         w_plane = sb.tile([P, PASSES, R], U8, name="w_plane", align_bytes=64)

@@ -91,7 +91,7 @@ def tile_list_largerpicks_relooked_rowpeaks_kernel(
                 w_codes[:].bitcast(U16).rearrange("p a (t m) -> p a t m", t=PACK),
                 w_raw[:].bitcast(U16).rearrange("p a (m t) -> p a t m", t=PACK),
             )
-            nc.vector.tensor_copy(
+            nc.gpsimd.tensor_copy(
                 w_plane[:].rearrange("p a (t m) -> p a t m", t=PACK),
                 ws_raw[:].rearrange("p a (m t) -> p a t m", t=PACK),
             )

from contextlib import ExitStack

import concourse.mybir as mybir

K, T, J, R, O, N = 1024, 1024, 256, 512, 128, 256
FLOPS = 2 * K * R * J + 2 * R * O * N

F32 = mybir.dt.float32
BF16 = mybir.dt.bfloat16
I32 = mybir.dt.int32
U32 = mybir.dt.uint32
U16 = mybir.dt.uint16
U8 = mybir.dt.uint8
E4M3 = mybir.dt.float8_e4m3fn_x4
E5M2 = mybir.dt.float8_e5m2_x4
E2M1 = mybir.dt.float4_e2m1fn_x4
ALU = mybir.AluOpType
ACT = mybir.ActivationFunctionType
X = mybir.AxisListType.X

P = 128
PACK = 4
PASSES = K // (P * PACK)
HALVES = 2
JH = J // HALVES
NH = N // HALVES
STRIPE = 16
JOINT = [3,3]
REUSE = {"pick1_01":"pick2_00","pick1_02":"pick1_00","late03":"pick2_02","early1":"pick2_02","pick1_11":"u0","late13":"pick2_12"}
SHARE = [256,256,128,0,0,256,0,0]


def tile_list_largerpicks_relooked_rowpeaks_kernel(
    tc, xf, fk, w_words, w_scales, wb_words, wb_scales, rs, offs, offs2, offs3, out
):
    nc = tc.nc
    with ExitStack() as ctx:
        sb = ctx.enter_context(tc.tile_pool(name="sb", bufs=1))
        psum = ctx.enter_context(tc.psum_pool(name="psum", bufs=1))

        list1 = sb.tile([P, J // STRIPE], U16, name="list1")
        list2 = sb.tile([P, J // STRIPE], U16, name="list2")
        list3 = sb.tile([P, O // STRIPE], U16, name="list3")
        planes = [(a, t) for a in range(PASSES) for t in range(PACK)]
        x_rows = xf.rearrange("(a p t) c -> a t p c", a=PASSES, t=PACK)
        x = {at: sb.tile([P, T], F32, name="x%d%d" % at) for at in planes}
        w_raw = sb.tile([P, PASSES, 2 * R], U8, name="w_raw", align_bytes=64)
        wb_codes = sb.tile([P, PACK * N], U8, name="wb_codes", align_bytes=64)
        rs_raw = sb.tile([P, N], F32, name="rs_raw")
        factor = sb.tile([P, PASSES, PACK], F32, name="factor")
        ws_raw = sb.tile([P, PASSES, R], U8, name="ws_raw", align_bytes=64)
        wb_plane = sb.tile([P, N], U8, name="wb_plane", align_bytes=64)

        def tile(shape, dtype, name):
            return sb.tile(shape, dtype, name=name, tag=REUSE.get(name, name), align_bytes=64)

        def load_plane(at):
            nc.sync.dma_start(x[at][:], x_rows[at[0], at[1]])

        warm_in = sb.tile([P, 1], F32, name="warm_in")
        warm_out = sb.tile([P, 1], F32, name="warm_out")
        nc.vector.memset(warm_in[:], 0.0)
        nc.scalar.activation(warm_out[:], warm_in[:], ACT.Copy)
        nc.vector.memset(ws_raw[:].bitcast(I32), 0)
        nc.vector.memset(wb_plane[:].bitcast(I32), 0)

        nc.sync.dma_start(list1[:], offs)
        nc.sync.dma_start(list2[:], offs2)
        load_plane(planes[0])
        nc.sync.dma_start(w_raw[:].bitcast(I32), w_words.rearrange("a p b -> p a b").bitcast(I32))
        for r in range(4):
            nc.sync.dma_start(
                ws_raw[r:P:32].bitcast(I32),
                w_scales[:, r:16:4, :].rearrange("a q c -> q a c").bitcast(I32),
            )
        nc.sync.dma_start(factor[:], fk.rearrange("(a p t) o -> p a (t o)", a=PASSES, t=PACK))
        for at in planes[1:]:
            load_plane(at)
        nc.sync.dma_start(list3[:], offs3)
        nc.sync.dma_start(rs_raw[:], rs)
        nc.sync.dma_start(wb_codes[:].bitcast(I32), wb_words[0].rearrange("p n t -> p (n t)").bitcast(I32))

        for r in range(4):
            nc.sync.dma_start(wb_plane[r:P:32].bitcast(I32), wb_scales[0, r:16:4, :].bitcast(I32))

        w_codes = sb.tile([P, PASSES, 2 * R], U8, name="w_codes", align_bytes=64)
        w_plane = sb.tile([P, PASSES, R], U8, name="w_plane", align_bytes=64)

        def deal_weights():
            nc.vector.tensor_copy(
                w_codes[:].bitcast(U16).rearrange("p a (t m) -> p a t m", t=PACK),
                w_raw[:].bitcast(U16).rearrange("p a (m t) -> p a t m", t=PACK),
            )
            nc.gpsimd.tensor_copy(
                w_plane[:].rearrange("p a (t m) -> p a t m", t=PACK),
                ws_raw[:].rearrange("p a (m t) -> p a t m", t=PACK),
            )

        def gather(engine_is_vector, picked, window, offsets, lo, hi):
            source = window[:].indirect(offsets[:, lo // STRIPE : hi // STRIPE])
            if engine_is_vector:
                nc.vector.tensor_copy(picked[:, lo:hi], source)
            else:
                nc.scalar.activation(picked[:, lo:hi], source, ACT.Copy)

        acc = [psum.tile([P, J], F32, name="acc%d" % t) for t in range(PACK)]
        for a in range(PASSES):
            u = tile([P, J, PACK], BF16, "u%d" % a)
            u_codes = sb.tile([P, J], U32, name="u_codes%d" % a, align_bytes=64)
            u_plane = sb.tile([P, J], U8, name="u_plane%d" % a, align_bytes=64)
            last_pass = a == PASSES - 1
            joint = JOINT[a]
            early = tile([P, joint, J], F32, "early%d" % a)
            for t in range(PACK):
                window = x[(a, t)]
                pick1 = tile([P, J], F32, "pick1_%d%d" % (a, t))
                pick2 = tile([P, J], F32, "pick2_%d%d" % (a, t))
                larger = early[:, t, :] if t < joint else tile([P, J], F32, "late%d%d" % (a, t))[:]
                share = SHARE[PACK * a + t]
                parts = [(0, JH), (JH, J)] if last_pass and t == PACK - 1 else [(0, J)]
                if share:
                    gather(True, pick1, window, list1, 0, share)
                for lo, hi in parts:
                    gather(False, pick2, window, list2, lo, hi)
                    if max(lo, share) < hi:
                        gather(False, pick1, window, list1, max(lo, share), hi)
                for lo, hi in parts:
                    nc.vector.tensor_tensor(larger[:, lo:hi], pick1[:, lo:hi], pick2[:, lo:hi], ALU.max)
                if t == joint - 1:
                    nc.vector.tensor_tensor(
                        u[:, :, :joint].rearrange("p (c i) t -> p c t i", i=4),
                        early[:].rearrange("p t (c i) -> p c t i", i=4),
                        factor[:, a, :joint].unsqueeze(1).unsqueeze(3).broadcast_to([P, J // 4, joint, 4]),
                        ALU.mult,
                    )
                if t >= joint:
                    for lo, hi in parts:
                        nc.vector.tensor_scalar(u[:, lo:hi, t], larger[:, lo:hi], factor[:, a, t : t + 1], None, ALU.mult)
                if (a, t) == planes[0]:
                    deal_weights()
            parts = [(0, JH), (JH, J)] if last_pass else [(0, J)]
            for lo, hi in parts:
                nc.vector.quantize_mx(
                    u_codes[:, lo:hi].bitcast(E4M3), u_plane[:, lo:hi], u[:, lo:hi, :].rearrange("p j t -> p (j t)")
                )
            for t in range(PACK):
                for lo, hi in parts:
                    nc.tensor.matmul_mx(
                        acc[t][:, lo:hi],
                        lhsT=w_codes[:, a, 2 * P * t : 2 * P * (t + 1)].bitcast(E2M1),
                        lhsT_scale=w_plane[:, a, P * t : P * (t + 1)],
                        rhs=u_codes[:, lo:hi].bitcast(E4M3),
                        rhs_scale=u_plane[:, lo:hi],
                        start=(a == 0),
                        stop=(last_pass and hi == J),
                    )

        residual = sb.tile([P, N], F32, name="residual")
        nc.scalar.activation(residual[:], rs_raw[:], ACT.Copy, scale=0.3)

        hid = sb.tile([P, O, PACK], BF16, name="hid", align_bytes=64)
        for t in range(PACK):
            ha = sb.tile([P, J], F32, name="ha%d" % t)
            nc.scalar.activation(ha[:], acc[t][:], ACT.Relu)
            nc.vector.tensor_copy(hid[:, :, t], ha[:].indirect(list3[:]))
        hid_codes = sb.tile([P, O], U32, name="hid_codes", align_bytes=64)
        hid_plane = sb.tile([P, O], U8, name="hid_plane", align_bytes=64)
        nc.vector.quantize_mx(hid_codes[:].bitcast(E5M2), hid_plane[:], hid[:].rearrange("p o t -> p (o t)"))

        prod = [psum.tile([P, NH], F32, name="prod%d" % h) for h in range(HALVES)]
        for h in range(HALVES):
            nc.tensor.matmul_mx(
                prod[h][:],
                lhsT=hid_codes[:].bitcast(E5M2),
                lhsT_scale=hid_plane[:],
                rhs=wb_codes[:].bitcast(U32)[:, h * NH : (h + 1) * NH].bitcast(E4M3),
                rhs_scale=wb_plane[:, h * NH : (h + 1) * NH],
                start=True,
                stop=True,
            )
        sizes = sb.tile([P, NH + 2], F32, name="sizes")
        nc.vector.tensor_reduce(sizes[:, NH : NH + 1], prod[0][:], X, ALU.max)
        nc.vector.tensor_reduce(sizes[:, NH + 1 : NH + 2], prod[0][:], X, ALU.min, negate=True)
        nc.scalar.activation(sizes[:, :NH], prod[1][:], ACT.Abs)
        shifted = sb.tile([P, NH + 2], F32, name="shifted")
        denom = sb.tile([P, 1], F32, name="denom")
        nc.vector.tensor_scalar(shifted[:], sizes[:], 0.2, None, ALU.add, ALU.max, accum_out=denom[:])
        inv = sb.tile([P, 1], F32, name="inv")
        nc.vector.reciprocal(inv[:], denom[:])
        result = sb.tile([P, N], F32, name="result")
        for h in range(HALVES):
            cols = slice(h * NH, (h + 1) * NH)
            nc.vector.scalar_tensor_tensor(result[:, cols], prod[h][:], inv[:], residual[:, cols], ALU.mult, ALU.add)
        nc.sync.dma_start(out, result[:])
